import numpy as np
import ml_dtypes


def mxq(x, axis, fmt="e4m3"):
    dtype, down = {"e4m3": (ml_dtypes.float8_e4m3fn, 7), "e5m2": (ml_dtypes.float8_e5m2, 14)}[fmt]
    v = np.moveaxis(np.asarray(x, np.float32).astype(ml_dtypes.bfloat16).astype(np.float64), axis, -1)
    blocks = v.reshape(v.shape[:-1] + (-1, 32))
    amax = np.abs(blocks).max(-1, keepdims=True)
    byte = np.maximum(np.where(amax > 0, np.frexp(amax)[1] - 1 + 127, 0) - down, 1)
    scale = np.exp2(byte - 127.0)
    codes = (blocks / scale).astype(np.float32).astype(dtype).astype(np.float64)
    return np.moveaxis((codes * scale).reshape(v.shape), -1, axis)


WIDE = False


def mx_kscale(k):
    if not WIDE:
        return np.ones(k)
    levels = np.array([10, -10, 5, -5, 0])
    if k % 512:
        return np.exp2(np.random.permutation(np.resize(levels, k // 32))).repeat(32)
    a = np.empty((k // 512, 16))
    for p in range(k // 512):
        a[p, :8] = np.random.permutation(np.resize(levels, 8))
        for g in range(8):
            far = levels[np.abs(levels - a[p, g]) >= 10]
            a[p, g + 8] = far[np.random.randint(len(far))]
    return np.exp2(a.ravel()).repeat(32)


BF16 = ml_dtypes.bfloat16


def bf(x):
    return np.asarray(x, np.float32).astype(BF16)


def f64(x):
    return np.asarray(x).astype(np.float64)


B, D, E, Q = 8192, 1024, 512, 256


def huber_influence(r):
    return np.maximum(-1.0, np.minimum(1.0, r))


def draw0():
    s = mx_kscale(D)
    u = mx_kscale(B)
    return {"x": bf(np.random.standard_normal((B, D)) * s),
            "m": bf(np.random.standard_normal((D, E)) / np.sqrt(D) / s[:, None]),
            "b": bf(0.5 * np.random.standard_normal(E)),
            "y": bf(np.random.standard_normal((B, E))),
            "c": bf((1.0 + 0.1 * np.random.standard_normal(B)) * u),
            "z": bf(np.random.standard_normal((B, Q)) / u[:, None])}


def core(x, m, b, y, c, z):
    n = x.shape[0]
    r = (mxq(f64(x), 1, "e4m3") @ mxq(f64(m), 0, "e4m3")) + f64(b) - f64(y)
    psi = huber_influence(r)
    t = f64(c)[:, None] * psi
    return (mxq(f64(z), 0, "e4m3").T @ mxq(t, 0, "e4m3")) / np.sqrt(n)


def e4m3fn_bytes(y):
    return np.clip(np.asarray(y, np.float64), -448.0, 448.0).astype(np.float32).astype(ml_dtypes.float8_e4m3fn).view(np.uint8)


def e4m3fn_values(b):
    return np.asarray(b, np.uint8).view(ml_dtypes.float8_e4m3fn).astype(np.float64)


def setup_inputs():
    d = draw0()
    x0 = np.asarray(d['x']).astype(np.float64)
    s = (np.max(np.abs(x0), axis=(0,), keepdims=True) / 448.0).astype(np.float32)
    out = {}
    for k, v in d.items():
        if k == 'x':
            out['x_bytes'] = e4m3fn_bytes(x0 / s.astype(np.float64))
            out['x_scale'] = s
        else:
            out[k] = v
    return out


def reference(x_bytes, x_scale, m, b, y, c, z):
    return core(e4m3fn_values(x_bytes) * x_scale.astype(np.float64), m, b, y, c, z)

@@ -1,0 +1,230 @@
+import math
+from contextlib import ExitStack
+
+import concourse.mybir as mybir
+from concourse.masks import make_identity
+
+B, D, E, Q = 8192, 1024, 512, 256
+FLOPS = 2 * B * D * E + 2 * B * Q * E
+
+F32 = mybir.dt.float32
+BF16 = mybir.dt.bfloat16
+U32 = mybir.dt.uint32
+U8 = mybir.dt.uint8
+FP8 = mybir.dt.float8_e4m3fn
+FP8X4 = mybir.dt.float8_e4m3fn_x4
+ACT = mybir.ActivationFunctionType
+ALU = mybir.AluOpType
+
+P = 128
+PACK = 4
+PASS = P * PACK
+GROUPS = B // PASS
+XPASSES = D // PASS
+CHUNKS = E // P
+
+
+def interleave(copy, dst, src):
+    copy(
+        out=dst.rearrange("p (c i t) -> p c t i", i=4, t=PACK),
+        in_=src.rearrange("p t (c i) -> p c t i", i=4),
+    )
+
+
+def tile_iv4rechubermomentmatrix_t_kernel(tc, x_bytes, x_scale, m, b, y, c, z, out):
+    nc = tc.nc
+    x_rows = x_bytes.rearrange("(j p t) k -> j p (t k)", p=P, t=PACK)
+    y_rows = y.rearrange("(j p t) e -> j p t e", p=P, t=PACK)
+    z_rows = z.rearrange("(j p t) q -> j p t q", p=P, t=PACK)
+    m_rows = m.rearrange("(g p t) e -> g p t e", p=P, t=PACK)
+
+    with ExitStack() as ctx:
+        keep = ctx.enter_context(tc.tile_pool(name="keep", bufs=1))
+        work = ctx.enter_context(tc.tile_pool(name="work", bufs=2))
+        ring = ctx.enter_context(tc.psum_pool(name="ring", bufs=6))
+        sums = ctx.enter_context(tc.psum_pool(name="sums", bufs=1))
+        ctx.enter_context(tc.manual_schedule())
+
+        ident_f32 = keep.tile([P, P], F32)
+        ident_bf16 = keep.tile([P, P], BF16)
+        make_identity(nc, ident_f32[:])
+        make_identity(nc, ident_bf16[:])
+
+        xb, xw, xg, xq, xs, yt, zt, zg, zq, zs, wt, tv, tc_, tg, tq, ts = ({} for n in range(16))
+
+        def load_x(j):
+            xb[j] = work.tile([P, PACK * D], U8, name="x_fp8_bytes", bufs=3)
+            nc.sync.dma_start(out=xb[j][:], in_=x_rows[j])
+
+        def load_y(j):
+            yt[j] = work.tile([P, PACK, E], BF16, name="y_tile", bufs=3)
+            nc.sync.dma_start(out=yt[j][:], in_=y_rows[j])
+
+        def load_z(j):
+            zt[j] = work.tile([P, PACK, Q], BF16, name="z_tile", bufs=3)
+            nc.sync.dma_start(out=zt[j][:], in_=z_rows[j])
+
+        scale_raw = keep.tile([P, D], F32)
+        nc.sync.dma_start(out=scale_raw[:], in_=x_scale.rearrange("o k -> (o k)").partition_broadcast(P))
+        load_x(0)
+        m_raw = [keep.tile([P, PACK, E], BF16, name="m_raw%d" % g) for g in range(XPASSES)]
+        for g in range(XPASSES):
+            nc.sync.dma_start(out=m_raw[g][:], in_=m_rows[g])
+        load_x(1)
+        b_raw = keep.tile([P, CHUNKS, 2], BF16)
+        nc.sync.dma_start(out=b_raw[:, :, 0:1], in_=b.rearrange("(j p o) -> p j o", p=P, o=1), allow_slow_non_contiguous=True)
+        c_raw = keep.tile([P, GROUPS, PACK], BF16)
+        nc.sync.dma_start(out=c_raw[:], in_=c.rearrange("(j p t) -> p j t", p=P, t=PACK))
+
+        scale = keep.tile([P, 2, 2, D // 2], F32)
+        scale_src = scale_raw[:].rearrange("p (w u e) -> p u w e", u=2, e=2)
+        nc.vector.tensor_copy(out=scale[:, :, 0, :].rearrange("p u (w e) -> p u w e", e=2), in_=scale_src)
+        nc.scalar.copy(out=scale[:, :, 1, :].rearrange("p u (w e) -> p u w e", e=2), in_=scale_src)
+
+        m_codes = keep.tile([P, XPASSES, E], U32, align_bytes=64)
+        m_scales = keep.tile([P, XPASSES, E], U8, align_bytes=64)
+        m_grouped = [keep.tile([P, PACK * E], BF16, name="m_grouped%d" % g, align_bytes=64) for g in range(XPASSES)]
+        neg_b = keep.tile([P, CHUNKS], F32)
+        neg_c = keep.tile([P, GROUPS * PACK], F32)
+        hi_c = keep.tile([P, GROUPS * PACK], F32)
+        lo_c = keep.tile([P, GROUPS * PACK], F32)
+        moments = [sums.tile([P, E], F32, name="moment%d" % h) for h in range(Q // P)]
+
+        def prepare_m():
+            for g in range(XPASSES):
+                interleave(nc.scalar.copy, m_grouped[g][:], m_raw[g][:])
+
+        def quant_m():
+            for g in range(XPASSES):
+                nc.vector.quantize_mx(out=m_codes[:, g, :].bitcast(FP8X4), scales=m_scales[:, g, :], in_=m_grouped[g][:])
+
+        def prepare_small():
+            c_flat = c_raw[:].rearrange("p j t -> p (j t)")
+            nc.vector.tensor_scalar(out=neg_b[:], in0=b_raw[:, :, 0], scalar1=-1.0, scalar2=None, op0=ALU.mult)
+            nc.vector.tensor_scalar(out=neg_c[:], in0=c_flat, scalar1=-1.0, scalar2=None, op0=ALU.mult)
+            nc.vector.tensor_tensor(out=hi_c[:], in0=c_flat, in1=neg_c[:], op=ALU.max)
+            nc.vector.tensor_tensor(out=lo_c[:], in0=c_flat, in1=neg_c[:], op=ALU.min)
+
+        def widen(j, h):
+            xw[j, h] = work.tile([P, 2 * D], BF16, name="x_wide", bufs=4)
+            codes = xb[j][:, 2 * D * h : 2 * D * (h + 1)].bitcast(FP8)
+            nc.vector.tensor_tensor(
+                out=xw[j, h][:].rearrange("p (u w e) -> p u w e", u=2, e=2),
+                in0=codes.rearrange("p (w u e) -> p u w e", u=2, e=2),
+                in1=scale[:].rearrange("p u r (w e) -> p u (r w) e", e=2),
+                op=ALU.mult,
+            )
+
+        def turn_x(j, k):
+            g, h = divmod(k, 2)
+            if h == 0:
+                xg[j, g] = work.tile([P, PACK * PASS], BF16, name="x_grouped", bufs=4, align_bytes=64)
+            bank = ring.tile([P, 2, 2, P], F32, name="bank")
+            words = xw[j, h][:].bitcast(F32).rearrange("p (u r g w) -> p u r g w", u=2, r=2, g=XPASSES)
+            for r in range(2):
+                for u in range(2):
+                    nc.tensor.transpose(bank[:, r, u, :], words[:, u, r, g, :], ident_f32[:])
+            dst = xg[j, g][:, 2 * PASS * h : 2 * PASS * (h + 1)].bitcast(F32)
+            nc.scalar.copy(out=dst.rearrange("p (r n u) -> p r n u", r=2, u=2), in_=bank[:].rearrange("p r u n -> p r n u"))
+
+        def quant_x(j, g):
+            xq[j, g] = work.tile([P, PASS], U32, name="x_codes", bufs=4, align_bytes=64)
+            xs[j, g] = work.tile([P, PASS], U8, name="x_scales", bufs=4, align_bytes=64)
+            nc.vector.quantize_mx(out=xq[j, g][:].bitcast(FP8X4), scales=xs[j, g][:], in_=xg[j, g][:])
+
+        def predict(j, k):
+            bank = ring.tile([P, PASS], F32, name="bank")
+            cols = slice(P * k, P * (k + 1))
+            for g in range(XPASSES):
+                nc.tensor.matmul_mx(
+                    out=bank[:], lhsT=m_codes[:, g, cols].bitcast(FP8X4), lhsT_scale=m_scales[:, g, cols],
+                    rhs=xq[j, g][:].bitcast(FP8X4), rhs_scale=xs[j, g][:], start=(g == 0), stop=(g == XPASSES - 1),
+                )
+            wt[j, k] = work.tile([P, PASS], F32, name="pred_T", bufs=2 * CHUNKS)
+            nc.scalar.activation(out=wt[j, k][:], in_=bank[:], func=ACT.Identity, scale=-1.0, bias=neg_b[:, k : k + 1])
+
+        def residual(j, t):
+            bank = ring.tile([P, E], F32, name="bank")
+            nc.tensor.matmul(out=bank[:], lhsT=ident_bf16[:], rhs=yt[j][:, t, :], start=True, stop=False)
+            for k in range(CHUNKS):
+                nc.tensor.matmul(
+                    out=bank[:, P * k : P * (k + 1)], lhsT=wt[j, k][:, P * t : P * (t + 1)], rhs=ident_f32[:],
+                    is_transpose=True, start=False, stop=(k == CHUNKS - 1),
+                )
+            if t == 0:
+                tv[j] = work.tile([P, PACK, E], BF16, name="t_unclipped", bufs=2)
+            col = PACK * j + t
+            nc.scalar.activation(out=tv[j][:, t, :], in_=bank[:], func=ACT.Copy, scale=neg_c[:, col : col + 1])
+
+        def clip(j, t):
+            if t == 0:
+                tc_[j] = work.tile([P, PACK, E], BF16, name="t_clipped", bufs=2)
+            col = PACK * j + t
+            nc.vector.tensor_scalar(
+                out=tc_[j][:, t, :], in0=tv[j][:, t, :], scalar1=lo_c[:, col : col + 1], scalar2=hi_c[:, col : col + 1],
+                op0=ALU.max, op1=ALU.min,
+            )
+
+        def group_t(j):
+            tg[j] = work.tile([P, PACK * E], BF16, name="t_grouped", bufs=2, align_bytes=64)
+            interleave(nc.vector.tensor_copy, tg[j][:], tc_[j][:])
+
+        def quant_t(j):
+            tq[j] = work.tile([P, E], U32, name="t_codes", bufs=2, align_bytes=64)
+            ts[j] = work.tile([P, E], U8, name="t_scales", bufs=2, align_bytes=64)
+            nc.vector.quantize_mx(out=tq[j][:].bitcast(FP8X4), scales=ts[j][:], in_=tg[j][:])
+
+        def group_z(j):
+            zg[j] = work.tile([P, PACK * Q], BF16, name="z_grouped", bufs=2, align_bytes=64)
+            interleave(nc.scalar.copy, zg[j][:], zt[j][:])
+
+        def quant_z(j):
+            zq[j] = work.tile([P, Q], U32, name="z_codes", bufs=2, align_bytes=64)
+            zs[j] = work.tile([P, Q], U8, name="z_scales", bufs=2, align_bytes=64)
+            nc.vector.quantize_mx(out=zq[j][:].bitcast(FP8X4), scales=zs[j][:], in_=zg[j][:])
+
+        def moment(j):
+            for h in range(Q // P):
+                cols = slice(P * h, P * (h + 1))
+                nc.tensor.matmul_mx(
+                    out=moments[h][:], lhsT=zq[j][:, cols].bitcast(FP8X4), lhsT_scale=zs[j][:, cols],
+                    rhs=tq[j][:].bitcast(FP8X4), rhs_scale=ts[j][:], start=(j == 0), stop=(j == GROUPS - 1),
+                )
+
+        def at(fn, j, *rest):
+            if 0 <= j < GROUPS:
+                fn(j, *rest)
+
+        for s in range(GROUPS + 6):
+            if s > 0:
+                at(load_x, s + 1)
+            at(load_y, s - 2)
+            at(load_z, s - 3)
+            if s == 0:
+                prepare_m()
+            for k in range(4):
+                at(turn_x, s - 1, k)
+                at(predict, s - 3, k)
+                if k == 0:
+                    at(moment, s - 6)
+                at(residual, s - 4, k)
+            at(group_z, s - 4)
+            at(quant_x, s - 2, 0)
+            for t in range(PACK):
+                at(clip, s - 5, t)
+            at(quant_x, s - 2, 1)
+            at(widen, s, 0)
+            at(group_t, s - 5)
+            at(quant_z, s - 5)
+            at(widen, s, 1)
+            at(quant_t, s - 5)
+            if s == 1:
+                quant_m()
+                prepare_small()
+
+        result = keep.tile([P, Q // P, E], F32)
+        inv = 1.0 / math.sqrt(B)
+        nc.scalar.activation(out=result[:, 0, :], in_=moments[0][:], func=ACT.Copy, scale=inv)
+        nc.vector.tensor_scalar(out=result[:, 1, :], in0=moments[1][:], scalar1=inv, scalar2=None, op0=ALU.mult)
+        for h in range(Q // P):
+            nc.sync.dma_start(out=out[P * h : P * (h + 1), :], in_=result[:, h, :])

@@ -22,6 +22,11 @@ PASS = P * PACK
 GROUPS = B // PASS
 XPASSES = D // PASS
 CHUNKS = E // P
+RING = 3
+X3 = 1
+TAIL_V = 336
+LAG = 3
+POOL_Z = 192
 
 
 def interleave(copy, dst, src):
@@ -41,7 +46,8 @@ def tile_iv4rechubermomentmatrix_t_kernel(tc, x_bytes, x_scale, m, b, y, c, z, o
     with ExitStack() as ctx:
         keep = ctx.enter_context(tc.tile_pool(name="keep", bufs=1))
         work = ctx.enter_context(tc.tile_pool(name="work", bufs=2))
-        ring = ctx.enter_context(tc.psum_pool(name="ring", bufs=6))
+        ring = ctx.enter_context(tc.psum_pool(name="ring", bufs=RING))
+        xring = ctx.enter_context(tc.psum_pool(name="xring", bufs=6 - RING))
         sums = ctx.enter_context(tc.psum_pool(name="sums", bufs=1))
         ctx.enter_context(tc.manual_schedule())
 
@@ -50,7 +56,7 @@ def tile_iv4rechubermomentmatrix_t_kernel(tc, x_bytes, x_scale, m, b, y, c, z, o
         make_identity(nc, ident_f32[:])
         make_identity(nc, ident_bf16[:])
 
-        xb, xw, xg, xq, xs, yt, zt, zg, zq, zs, wt, tv, tc_, tg, tq, ts = ({} for n in range(16))
+        xb, xw, xg, xq, xs, yt, zt, zg, zq, zs, wt, tv, tc_, tg, tq, ts, xt = ({} for n in range(17))
 
         def load_x(j):
             xb[j] = work.tile([P, PACK * D], U8, name="x_fp8_bytes", bufs=3)
@@ -61,12 +67,13 @@ def tile_iv4rechubermomentmatrix_t_kernel(tc, x_bytes, x_scale, m, b, y, c, z, o
             nc.sync.dma_start(out=yt[j][:], in_=y_rows[j])
 
         def load_z(j):
-            zt[j] = work.tile([P, PACK, Q], BF16, name="z_tile", bufs=3)
-            nc.sync.dma_start(out=zt[j][:], in_=z_rows[j])
+            tc_[j] = work.tile([P, PACK, E + Q], BF16, name="tz_planes", bufs=3)
+            if j < GROUPS:
+                nc.sync.dma_start(out=tc_[j][:, :, E:], in_=z_rows[j])
 
-        scale_raw = keep.tile([P, D], F32)
-        nc.sync.dma_start(out=scale_raw[:], in_=x_scale.rearrange("o k -> (o k)").partition_broadcast(P))
+        scale_cols = keep.tile([P, XPASSES, PACK], F32)
         load_x(0)
+        nc.sync.dma_start(out=scale_cols[:], in_=x_scale.rearrange("o (g p t) -> p (o g) t", p=P, t=PACK))
         m_raw = [keep.tile([P, PACK, E], BF16, name="m_raw%d" % g) for g in range(XPASSES)]
         for g in range(XPASSES):
             nc.sync.dma_start(out=m_raw[g][:], in_=m_rows[g])
@@ -75,11 +82,6 @@ def tile_iv4rechubermomentmatrix_t_kernel(tc, x_bytes, x_scale, m, b, y, c, z, o
         nc.sync.dma_start(out=b_raw[:, :, 0:1], in_=b.rearrange("(j p o) -> p j o", p=P, o=1), allow_slow_non_contiguous=True)
         c_raw = keep.tile([P, GROUPS, PACK], BF16)
         nc.sync.dma_start(out=c_raw[:], in_=c.rearrange("(j p t) -> p j t", p=P, t=PACK))
-
-        scale = keep.tile([P, 2, 2, D // 2], F32)
-        scale_src = scale_raw[:].rearrange("p (w u e) -> p u w e", u=2, e=2)
-        nc.vector.tensor_copy(out=scale[:, :, 0, :].rearrange("p u (w e) -> p u w e", e=2), in_=scale_src)
-        nc.scalar.copy(out=scale[:, :, 1, :].rearrange("p u (w e) -> p u w e", e=2), in_=scale_src)
 
         m_codes = keep.tile([P, XPASSES, E], U32, align_bytes=64)
         m_scales = keep.tile([P, XPASSES, E], U8, align_bytes=64)
@@ -91,8 +93,8 @@ def tile_iv4rechubermomentmatrix_t_kernel(tc, x_bytes, x_scale, m, b, y, c, z, o
         moments = [sums.tile([P, E], F32, name="moment%d" % h) for h in range(Q // P)]
 
         def prepare_m():
-            for g in range(XPASSES):
-                interleave(nc.scalar.copy, m_grouped[g][:], m_raw[g][:])
+            interleave(nc.vector.tensor_copy, m_grouped[0][:], m_raw[0][:])
+            pool_interleave(m_grouped[1][:], m_raw[1][:])
 
         def quant_m():
             for g in range(XPASSES):
@@ -105,34 +107,48 @@ def tile_iv4rechubermomentmatrix_t_kernel(tc, x_bytes, x_scale, m, b, y, c, z, o
             nc.vector.tensor_tensor(out=hi_c[:], in0=c_flat, in1=neg_c[:], op=ALU.max)
             nc.vector.tensor_tensor(out=lo_c[:], in0=c_flat, in1=neg_c[:], op=ALU.min)
 
-        def widen(j, h):
-            xw[j, h] = work.tile([P, 2 * D], BF16, name="x_wide", bufs=4)
-            codes = xb[j][:, 2 * D * h : 2 * D * (h + 1)].bitcast(FP8)
-            nc.vector.tensor_tensor(
-                out=xw[j, h][:].rearrange("p (u w e) -> p u w e", u=2, e=2),
-                in0=codes.rearrange("p (w u e) -> p u w e", u=2, e=2),
-                in1=scale[:].rearrange("p u r (w e) -> p u (r w) e", e=2),
-                op=ALU.mult,
+        def widen(j, t, copy):
+            xw[j, t] = work.tile([P, D], BF16, name="x_wide", bufs=3 * PACK)
+            codes = xb[j][:, D * t : D * (t + 1)].bitcast(FP8)
+            copy(
+                out=xw[j, t][:].rearrange("p (u w e) -> p u w e", u=2, e=2),
+                in_=codes.rearrange("p (w u e) -> p u w e", u=2, e=2),
+            )
+
+        def widen_on_vector(j, t):
+            xw[j, t] = work.tile([P, D], BF16, name="x_wide", bufs=3 * PACK)
+            codes = xb[j][:, D * t : D * (t + 1)].bitcast(FP8)
+            nc.vector.tensor_copy(
+                out=xw[j, t][:].rearrange("p (u w e) -> p w u e", u=2, e=2),
+                in_=codes.rearrange("p (w u e) -> p w u e", u=2, e=2),
             )
 
         def turn_x(j, k):
-            g, h = divmod(k, 2)
+            h, g = divmod(k, 2)
+            xt[j, k] = xring.tile([P, 2, 2, P], F32, name="x_bank")
+            for r in range(2):
+                words = xw[j, 2 * h + r][:].bitcast(F32).rearrange("p (u g w) -> p u g w", u=2, g=XPASSES)
+                for u in range(2):
+                    nc.tensor.transpose(xt[j, k][:, u, r, :], words[:, u, g, :], ident_f32[:])
+
+        def scale_x(j, k):
+            h, g = divmod(k, 2)
             if h == 0:
                 xg[j, g] = work.tile([P, PACK * PASS], BF16, name="x_grouped", bufs=4, align_bytes=64)
-            bank = ring.tile([P, 2, 2, P], F32, name="bank")
-            words = xw[j, h][:].bitcast(F32).rearrange("p (u r g w) -> p u r g w", u=2, r=2, g=XPASSES)
-            for r in range(2):
-                for u in range(2):
-                    nc.tensor.transpose(bank[:, r, u, :], words[:, u, r, g, :], ident_f32[:])
-            dst = xg[j, g][:, 2 * PASS * h : 2 * PASS * (h + 1)].bitcast(F32)
-            nc.scalar.copy(out=dst.rearrange("p (r n u) -> p r n u", r=2, u=2), in_=bank[:].rearrange("p r u n -> p r n u"))
+            values = xt[j, k][:].rearrange("p u r n -> p (u r n)").bitcast(BF16)
+            nc.vector.tensor_tensor(
+                out=xg[j, g][:, 2 * PASS * h : 2 * PASS * (h + 1)].rearrange("p (n u e) -> p n u e", u=2, e=2),
+                in0=values.rearrange("p (u n e) -> p n u e", u=2, e=2),
+                in1=scale_cols[:, g, :].rearrange("p (u e) -> p u e", u=2).unsqueeze(1).to_broadcast([P, 2 * P, 2, 2]),
+                op=ALU.mult,
+            )
 
         def quant_x(j, g):
             xq[j, g] = work.tile([P, PASS], U32, name="x_codes", bufs=4, align_bytes=64)
             xs[j, g] = work.tile([P, PASS], U8, name="x_scales", bufs=4, align_bytes=64)
             nc.vector.quantize_mx(out=xq[j, g][:].bitcast(FP8X4), scales=xs[j, g][:], in_=xg[j, g][:])
 
-        def predict(j, k):
+        def predict(j, k, on_vector=False):
             bank = ring.tile([P, PASS], F32, name="bank")
             cols = slice(P * k, P * (k + 1))
             for g in range(XPASSES):
@@ -141,9 +157,12 @@ def tile_iv4rechubermomentmatrix_t_kernel(tc, x_bytes, x_scale, m, b, y, c, z, o
                     rhs=xq[j, g][:].bitcast(FP8X4), rhs_scale=xs[j, g][:], start=(g == 0), stop=(g == XPASSES - 1),
                 )
             wt[j, k] = work.tile([P, PASS], F32, name="pred_T", bufs=2 * CHUNKS)
-            nc.scalar.activation(out=wt[j, k][:], in_=bank[:], func=ACT.Identity, scale=-1.0, bias=neg_b[:, k : k + 1])
+            if on_vector:
+                nc.vector.tensor_scalar(out=wt[j, k][:], in0=bank[:], scalar1=-1.0, scalar2=neg_b[:, k : k + 1], op0=ALU.mult, op1=ALU.add)
+            else:
+                nc.scalar.activation(out=wt[j, k][:], in_=bank[:], func=ACT.Identity, scale=-1.0, bias=neg_b[:, k : k + 1])
 
-        def residual(j, t):
+        def residual(j, t, on_vector=False):
             bank = ring.tile([P, E], F32, name="bank")
             nc.tensor.matmul(out=bank[:], lhsT=ident_bf16[:], rhs=yt[j][:, t, :], start=True, stop=False)
             for k in range(CHUNKS):
@@ -154,34 +173,45 @@ def tile_iv4rechubermomentmatrix_t_kernel(tc, x_bytes, x_scale, m, b, y, c, z, o
             if t == 0:
                 tv[j] = work.tile([P, PACK, E], BF16, name="t_unclipped", bufs=2)
             col = PACK * j + t
-            nc.scalar.activation(out=tv[j][:, t, :], in_=bank[:], func=ACT.Copy, scale=neg_c[:, col : col + 1])
+            if on_vector:
+                nc.vector.tensor_scalar(out=tv[j][:, t, :], in0=bank[:], scalar1=neg_c[:, col : col + 1], scalar2=None, op0=ALU.mult)
+            else:
+                nc.scalar.activation(out=tv[j][:, t, :], in_=bank[:], func=ACT.Copy, scale=neg_c[:, col : col + 1])
 
         def clip(j, t):
-            if t == 0:
-                tc_[j] = work.tile([P, PACK, E], BF16, name="t_clipped", bufs=2)
             col = PACK * j + t
             nc.vector.tensor_scalar(
-                out=tc_[j][:, t, :], in0=tv[j][:, t, :], scalar1=lo_c[:, col : col + 1], scalar2=hi_c[:, col : col + 1],
+                out=tc_[j + LAG][:, t, :E], in0=tv[j][:, t, :], scalar1=lo_c[:, col : col + 1], scalar2=hi_c[:, col : col + 1],
                 op0=ALU.max, op1=ALU.min,
             )
 
-        def group_t(j):
-            tg[j] = work.tile([P, PACK * E], BF16, name="t_grouped", bufs=2, align_bytes=64)
-            interleave(nc.vector.tensor_copy, tg[j][:], tc_[j][:])
+        def pool_interleave(dst, src):
+            nc.gpsimd.tensor_scalar(
+                out=dst.rearrange("p (c t) -> p c t", t=PACK), in0=src.rearrange("p t c -> p c t"),
+                scalar1=1.0, scalar2=0.0, op0=ALU.mult, op1=ALU.add,
+            )
+
+        def group_tz(j, how, lo, hi):
+            if j not in tg:
+                tg[j] = work.tile([P, PACK * (E + Q)], BF16, name="tz_grouped", bufs=2, align_bytes=64)
+            if lo < hi:
+                how(tg[j][:, PACK * lo : PACK * hi], tc_[j][:, :, lo:hi])
+
+        def vector_interleave(dst, src):
+            interleave(nc.vector.tensor_copy, dst, src)
+
+        def scalar_interleave(dst, src):
+            interleave(nc.scalar.copy, dst, src)
 
         def quant_t(j):
             tq[j] = work.tile([P, E], U32, name="t_codes", bufs=2, align_bytes=64)
             ts[j] = work.tile([P, E], U8, name="t_scales", bufs=2, align_bytes=64)
-            nc.vector.quantize_mx(out=tq[j][:].bitcast(FP8X4), scales=ts[j][:], in_=tg[j][:])
-
-        def group_z(j):
-            zg[j] = work.tile([P, PACK * Q], BF16, name="z_grouped", bufs=2, align_bytes=64)
-            interleave(nc.scalar.copy, zg[j][:], zt[j][:])
+            nc.vector.quantize_mx(out=tq[j][:].bitcast(FP8X4), scales=ts[j][:], in_=tg[j + LAG][:, : PACK * E])
 
         def quant_z(j):
-            zq[j] = work.tile([P, Q], U32, name="z_codes", bufs=2, align_bytes=64)
-            zs[j] = work.tile([P, Q], U8, name="z_scales", bufs=2, align_bytes=64)
-            nc.vector.quantize_mx(out=zq[j][:].bitcast(FP8X4), scales=zs[j][:], in_=zg[j][:])
+            zq[j] = work.tile([P, Q], U32, name="z_codes", bufs=LAG + 3, align_bytes=64)
+            zs[j] = work.tile([P, Q], U8, name="z_scales", bufs=LAG + 3, align_bytes=64)
+            nc.vector.quantize_mx(out=zq[j][:].bitcast(FP8X4), scales=zs[j][:], in_=tg[j][:, PACK * E :])
 
         def moment(j):
             for h in range(Q // P):
@@ -195,32 +225,83 @@ def tile_iv4rechubermomentmatrix_t_kernel(tc, x_bytes, x_scale, m, b, y, c, z, o
             if 0 <= j < GROUPS:
                 fn(j, *rest)
 
-        for s in range(GROUPS + 6):
+        load_z(0)
+        load_x(2)
+        for t in range(PACK):
+            if t % 2 == 0:
+                widen(0, t, nc.scalar.copy)
+            else:
+                widen_on_vector(0, t)
+        for k in range(3):
+            turn_x(0, k)
+        for t in range(PACK):
+            widen(1, t, nc.scalar.copy)
+        for s in range(GROUPS):
             if s > 0:
-                at(load_x, s + 1)
-            at(load_y, s - 2)
-            at(load_z, s - 3)
+                at(load_x, s + 2)
+            at(load_y, s - 1)
+            load_z(s + 1)
+            for t in range(PACK):
+                at(clip, s - LAG, t)
             if s == 0:
                 prepare_m()
+            group_tz(s, pool_interleave, 0 if s >= LAG else E, E + POOL_Z if s > 0 else E)
+            for k in range(3):
+                at(scale_x, s, k)
             for k in range(4):
-                at(turn_x, s - 1, k)
-                at(predict, s - 3, k)
+                at(predict, s - 1, k)
+                if k == 1:
+                    at(moment, s - LAG - 1)
+                at(residual, s - 2, k)
                 if k == 0:
-                    at(moment, s - 6)
-                at(residual, s - 4, k)
-            at(group_z, s - 4)
-            at(quant_x, s - 2, 0)
-            for t in range(PACK):
-                at(clip, s - 5, t)
-            at(quant_x, s - 2, 1)
-            at(widen, s, 0)
-            at(group_t, s - 5)
-            at(quant_z, s - 5)
-            at(widen, s, 1)
-            at(quant_t, s - 5)
-            if s == 1:
+                    at(group_tz, s, scalar_interleave, E + POOL_Z if s > 0 else E, E + Q)
+                if k == X3:
+                    at(turn_x, s, 3)
+                    at(scale_x, s, 3)
+                at(widen, s + 2, k, nc.scalar.copy)
+            for k in range(3):
+                at(turn_x, s + 1, k)
+            if s == 0:
                 quant_m()
                 prepare_small()
+            at(quant_x, s, 0)
+            at(quant_x, s, 1)
+            at(quant_t, s - LAG)
+            at(quant_z, s)
+
+        last = GROUPS - 1
+        load_y(last)
+        load_z(GROUPS + 1)
+        for t in range(PACK):
+            clip(last - 2, t)
+        residual(last - 1, 0)
+        residual(last - 1, 1)
+        group_tz(GROUPS, vector_interleave, 0, E)
+        for k in range(CHUNKS):
+            predict(last, k, k == 2)
+        moment(last - 3)
+        quant_t(last - 2)
+        residual(last - 1, 2)
+        residual(last - 1, 3)
+        for t in range(PACK):
+            clip(last - 1, t)
+        load_z(GROUPS + 2)
+        moment(last - 2)
+        residual(last, 0)
+        group_tz(GROUPS + 1, vector_interleave, 0, E)
+        residual(last, 1)
+        clip(last, 0)
+        quant_t(last - 1)
+        residual(last, 2)
+        clip(last, 1)
+        residual(last, 3, True)
+        moment(last - 1)
+        clip(last, 2)
+        clip(last, 3)
+        group_tz(GROUPS + 2, vector_interleave, 0, TAIL_V)
+        group_tz(GROUPS + 2, scalar_interleave, TAIL_V, E)
+        quant_t(last)
+        moment(last)
 
         result = keep.tile([P, Q // P, E], F32)
         inv = 1.0 / math.sqrt(B)

@@ -23,10 +23,10 @@ GROUPS = B // PASS
 XPASSES = D // PASS
 CHUNKS = E // P
 RING = 3
-X3 = 1
 TAIL_V = 336
-LAG = 3
-POOL_Z = 192
+LAG = 2
+POOL_Z = 224
+WB = 2
 
 
 def interleave(copy, dst, src):
@@ -66,10 +66,13 @@ def tile_iv4rechubermomentmatrix_t_kernel(tc, x_bytes, x_scale, m, b, y, c, z, o
             yt[j] = work.tile([P, PACK, E], BF16, name="y_tile", bufs=3)
             nc.sync.dma_start(out=yt[j][:], in_=y_rows[j])
 
-        def load_z(j):
-            tc_[j] = work.tile([P, PACK, E + Q], BF16, name="tz_planes", bufs=3)
-            if j < GROUPS:
-                nc.sync.dma_start(out=tc_[j][:, :, E:], in_=z_rows[j])
+        def load_z(s):
+            tc_[s] = work.tile([P, PACK, E + Q], BF16, name="tz_planes", bufs=3)
+            if s == 1:
+                for j in range(2):
+                    nc.sync.dma_start(out=tc_[s][:, :, Q * j : Q * (j + 1)], in_=z_rows[j])
+            if s + 1 < GROUPS:
+                nc.sync.dma_start(out=tc_[s][:, :, E:], in_=z_rows[s + 1])
 
         scale_cols = keep.tile([P, XPASSES, PACK], F32)
         load_x(0)
@@ -80,56 +83,54 @@ def tile_iv4rechubermomentmatrix_t_kernel(tc, x_bytes, x_scale, m, b, y, c, z, o
         load_x(1)
         b_raw = keep.tile([P, CHUNKS, 2], BF16)
         nc.sync.dma_start(out=b_raw[:, :, 0:1], in_=b.rearrange("(j p o) -> p j o", p=P, o=1), allow_slow_non_contiguous=True)
+        load_x(2)
+        load_z(1)
         c_raw = keep.tile([P, GROUPS, PACK], BF16)
         nc.sync.dma_start(out=c_raw[:], in_=c.rearrange("(j p t) -> p j t", p=P, t=PACK))
 
         m_codes = keep.tile([P, XPASSES, E], U32, align_bytes=64)
         m_scales = keep.tile([P, XPASSES, E], U8, align_bytes=64)
-        m_grouped = [keep.tile([P, PACK * E], BF16, name="m_grouped%d" % g, align_bytes=64) for g in range(XPASSES)]
+        m_grouped = [work.tile([P, PACK * E], BF16, name="tz_grouped", bufs=2, align_bytes=64) for g in range(XPASSES)]
         neg_b = keep.tile([P, CHUNKS], F32)
         neg_c = keep.tile([P, GROUPS * PACK], F32)
         hi_c = keep.tile([P, GROUPS * PACK], F32)
         lo_c = keep.tile([P, GROUPS * PACK], F32)
         moments = [sums.tile([P, E], F32, name="moment%d" % h) for h in range(Q // P)]
 
-        def prepare_m():
-            interleave(nc.vector.tensor_copy, m_grouped[0][:], m_raw[0][:])
-            pool_interleave(m_grouped[1][:], m_raw[1][:])
-
         def quant_m():
-            for g in range(XPASSES):
+            for g in reversed(range(XPASSES)):
                 nc.vector.quantize_mx(out=m_codes[:, g, :].bitcast(FP8X4), scales=m_scales[:, g, :], in_=m_grouped[g][:])
 
         def prepare_small():
             c_flat = c_raw[:].rearrange("p j t -> p (j t)")
-            nc.vector.tensor_scalar(out=neg_b[:], in0=b_raw[:, :, 0], scalar1=-1.0, scalar2=None, op0=ALU.mult)
-            nc.vector.tensor_scalar(out=neg_c[:], in0=c_flat, scalar1=-1.0, scalar2=None, op0=ALU.mult)
-            nc.vector.tensor_tensor(out=hi_c[:], in0=c_flat, in1=neg_c[:], op=ALU.max)
-            nc.vector.tensor_tensor(out=lo_c[:], in0=c_flat, in1=neg_c[:], op=ALU.min)
+            nc.scalar.activation(out=neg_b[:], in_=b_raw[:, :, 0], func=ACT.Copy, scale=-1.0)
+            nc.scalar.activation(out=neg_c[:], in_=c_flat, func=ACT.Copy, scale=-1.0)
+            nc.scalar.activation(out=hi_c[:], in_=c_flat, func=ACT.Abs)
+            nc.scalar.activation(out=lo_c[:], in_=hi_c[:], func=ACT.Copy, scale=-1.0)
 
-        def widen(j, t, copy):
-            xw[j, t] = work.tile([P, D], BF16, name="x_wide", bufs=3 * PACK)
-            codes = xb[j][:, D * t : D * (t + 1)].bitcast(FP8)
-            copy(
-                out=xw[j, t][:].rearrange("p (u w e) -> p u w e", u=2, e=2),
+        def widen(j, h):
+            xw[j, h] = work.tile([P, 2 * D], BF16, name="x_wide", bufs=6)
+            codes = xb[j][:, 2 * D * h : 2 * D * (h + 1)].bitcast(FP8)
+            nc.scalar.copy(
+                out=xw[j, h][:].rearrange("p (u w e) -> p u w e", u=2, e=2),
                 in_=codes.rearrange("p (w u e) -> p u w e", u=2, e=2),
             )
 
-        def widen_on_vector(j, t):
-            xw[j, t] = work.tile([P, D], BF16, name="x_wide", bufs=3 * PACK)
-            codes = xb[j][:, D * t : D * (t + 1)].bitcast(FP8)
+        def widen_on_vector(j, h):
+            xw[j, h] = work.tile([P, 2 * D], BF16, name="x_wide", bufs=6)
+            codes = xb[j][:, 2 * D * h : 2 * D * (h + 1)].bitcast(FP8)
             nc.vector.tensor_copy(
-                out=xw[j, t][:].rearrange("p (u w e) -> p w u e", u=2, e=2),
+                out=xw[j, h][:].rearrange("p (u w e) -> p w u e", u=2, e=2),
                 in_=codes.rearrange("p (w u e) -> p w u e", u=2, e=2),
             )
 
         def turn_x(j, k):
             h, g = divmod(k, 2)
             xt[j, k] = xring.tile([P, 2, 2, P], F32, name="x_bank")
-            for r in range(2):
-                words = xw[j, 2 * h + r][:].bitcast(F32).rearrange("p (u g w) -> p u g w", u=2, g=XPASSES)
-                for u in range(2):
-                    nc.tensor.transpose(xt[j, k][:, u, r, :], words[:, u, g, :], ident_f32[:])
+            words = xw[j, h][:].bitcast(F32).rearrange("p (u r g w) -> p u r g w", u=2, r=2, g=XPASSES)
+            for u in range(2):
+                for r in range(2):
+                    nc.tensor.transpose(xt[j, k][:, u, r, :], words[:, u, r, g, :], ident_f32[:])
 
         def scale_x(j, k):
             h, g = divmod(k, 2)
@@ -143,24 +144,43 @@ def tile_iv4rechubermomentmatrix_t_kernel(tc, x_bytes, x_scale, m, b, y, c, z, o
                 op=ALU.mult,
             )
 
-        def quant_x(j, g):
-            xq[j, g] = work.tile([P, PASS], U32, name="x_codes", bufs=4, align_bytes=64)
-            xs[j, g] = work.tile([P, PASS], U8, name="x_scales", bufs=4, align_bytes=64)
-            nc.vector.quantize_mx(out=xq[j, g][:].bitcast(FP8X4), scales=xs[j, g][:], in_=xg[j, g][:])
+        def quant_x(j, g, lo=0, hi=PASS):
+            if lo == 0:
+                xq[j, g] = work.tile([P, PASS], U32, name="x_codes", bufs=4, align_bytes=64)
+                xs[j, g] = work.tile([P, PASS], U8, name="x_scales", bufs=4, align_bytes=64)
+            nc.vector.quantize_mx(out=xq[j, g][:, lo:hi].bitcast(FP8X4), scales=xs[j, g][:, lo:hi], in_=xg[j, g][:, PACK * lo : PACK * hi])
 
-        def predict(j, k, on_vector=False):
-            bank = ring.tile([P, PASS], F32, name="bank")
+        def predict_into(bank, j, k, lo, hi):
             cols = slice(P * k, P * (k + 1))
             for g in range(XPASSES):
                 nc.tensor.matmul_mx(
-                    out=bank[:], lhsT=m_codes[:, g, cols].bitcast(FP8X4), lhsT_scale=m_scales[:, g, cols],
-                    rhs=xq[j, g][:].bitcast(FP8X4), rhs_scale=xs[j, g][:], start=(g == 0), stop=(g == XPASSES - 1),
+                    out=bank, lhsT=m_codes[:, g, cols].bitcast(FP8X4), lhsT_scale=m_scales[:, g, cols],
+                    rhs=xq[j, g][:, lo:hi].bitcast(FP8X4), rhs_scale=xs[j, g][:, lo:hi], start=(g == 0), stop=(g == XPASSES - 1),
                 )
-            wt[j, k] = work.tile([P, PASS], F32, name="pred_T", bufs=2 * CHUNKS)
+
+        def add_bias(bank, j, k, lo, hi, on_vector):
+            if lo == 0:
+                wt[j, k] = work.tile([P, PASS], F32, name="pred_T", bufs=2 * CHUNKS)
             if on_vector:
-                nc.vector.tensor_scalar(out=wt[j, k][:], in0=bank[:], scalar1=-1.0, scalar2=neg_b[:, k : k + 1], op0=ALU.mult, op1=ALU.add)
+                nc.vector.tensor_scalar(out=wt[j, k][:, lo:hi], in0=bank, scalar1=-1.0, scalar2=neg_b[:, k : k + 1], op0=ALU.mult, op1=ALU.add)
             else:
-                nc.scalar.activation(out=wt[j, k][:], in_=bank[:], func=ACT.Identity, scale=-1.0, bias=neg_b[:, k : k + 1])
+                nc.scalar.activation(out=wt[j, k][:, lo:hi], in_=bank, func=ACT.Identity, scale=-1.0, bias=neg_b[:, k : k + 1])
+
+        def predict(j, k):
+            bank = ring.tile([P, PASS], F32, name="bank")
+            predict_into(bank[:], j, k, 0, PASS)
+            add_bias(bank[:], j, k, 0, PASS, False)
+
+        def predict_half(j, h, pair, on_vector):
+            half = PASS // 2
+            if h == 0:
+                bank = ring.tile([P, 2, half], F32, name="bank")
+            else:
+                bank = xring.tile([P, 2, half], F32, name="x_bank")
+            for i in range(2):
+                predict_into(bank[:, i, :], j, 2 * pair + i, half * h, half * (h + 1))
+            for i in range(2):
+                add_bias(bank[:, i, :], j, 2 * pair + i, half * h, half * (h + 1), on_vector)
 
         def residual(j, t, on_vector=False):
             bank = ring.tile([P, E], F32, name="bank")
@@ -204,104 +224,127 @@ def tile_iv4rechubermomentmatrix_t_kernel(tc, x_bytes, x_scale, m, b, y, c, z, o
             interleave(nc.scalar.copy, dst, src)
 
         def quant_t(j):
-            tq[j] = work.tile([P, E], U32, name="t_codes", bufs=2, align_bytes=64)
-            ts[j] = work.tile([P, E], U8, name="t_scales", bufs=2, align_bytes=64)
+            tq[j] = work.tile([P, E], U32, name="t_codes", bufs=4, align_bytes=64)
+            ts[j] = work.tile([P, E], U8, name="t_scales", bufs=4, align_bytes=64)
             nc.vector.quantize_mx(out=tq[j][:].bitcast(FP8X4), scales=ts[j][:], in_=tg[j + LAG][:, : PACK * E])
 
-        def quant_z(j):
-            zq[j] = work.tile([P, Q], U32, name="z_codes", bufs=LAG + 3, align_bytes=64)
-            zs[j] = work.tile([P, Q], U8, name="z_scales", bufs=LAG + 3, align_bytes=64)
-            nc.vector.quantize_mx(out=zq[j][:].bitcast(FP8X4), scales=zs[j][:], in_=tg[j][:, PACK * E :])
+        def quant_z(j, s, lo):
+            zq[j] = work.tile([P, Q], U32, name="z_codes", bufs=7, align_bytes=64)
+            zs[j] = work.tile([P, Q], U8, name="z_scales", bufs=7, align_bytes=64)
+            nc.vector.quantize_mx(out=zq[j][:].bitcast(FP8X4), scales=zs[j][:], in_=tg[s][:, PACK * lo : PACK * (lo + Q)])
 
-        def moment(j):
-            for h in range(Q // P):
-                cols = slice(P * h, P * (h + 1))
-                nc.tensor.matmul_mx(
-                    out=moments[h][:], lhsT=zq[j][:, cols].bitcast(FP8X4), lhsT_scale=zs[j][:, cols],
-                    rhs=tq[j][:].bitcast(FP8X4), rhs_scale=ts[j][:], start=(j == 0), stop=(j == GROUPS - 1),
-                )
+        def moment(j, h):
+            cols = slice(P * h, P * (h + 1))
+            nc.tensor.matmul_mx(
+                out=moments[h][:], lhsT=zq[j][:, cols].bitcast(FP8X4), lhsT_scale=zs[j][:, cols],
+                rhs=tq[j][:].bitcast(FP8X4), rhs_scale=ts[j][:], start=(j == 0), stop=(j == GROUPS - 1),
+            )
 
         def at(fn, j, *rest):
             if 0 <= j < GROUPS:
                 fn(j, *rest)
 
-        load_z(0)
-        load_x(2)
-        for t in range(PACK):
-            if t % 2 == 0:
-                widen(0, t, nc.scalar.copy)
-            else:
-                widen_on_vector(0, t)
-        for k in range(3):
-            turn_x(0, k)
-        for t in range(PACK):
-            widen(1, t, nc.scalar.copy)
-        for s in range(GROUPS):
+        widen(0, 0)
+        widen_on_vector(0, 1)
+        turn_x(0, 0)
+        turn_x(0, 1)
+        scalar_interleave(m_grouped[0][:], m_raw[0][:])
+        pool_interleave(m_grouped[1][:], m_raw[1][:])
+        last = GROUPS - 1
+        for s in range(last):
+            load_y(s)
             if s > 0:
+                load_z(s + 1)
                 at(load_x, s + 2)
-            at(load_y, s - 1)
-            load_z(s + 1)
             for t in range(PACK):
                 at(clip, s - LAG, t)
-            if s == 0:
-                prepare_m()
-            group_tz(s, pool_interleave, 0 if s >= LAG else E, E + POOL_Z if s > 0 else E)
-            for k in range(3):
-                at(scale_x, s, k)
-            for k in range(4):
+            if s > 0:
+                group_tz(s, pool_interleave, 0, E + POOL_Z)
+            scale_x(s, 0)
+            if s <= 1:
+                turn_x(s, 2)
+            for k in range(CHUNKS):
                 at(predict, s - 1, k)
-                if k == 1:
-                    at(moment, s - LAG - 1)
-                at(residual, s - 2, k)
-                if k == 0:
-                    at(group_tz, s, scalar_interleave, E + POOL_Z if s > 0 else E, E + Q)
-                if k == X3:
-                    at(turn_x, s, 3)
-                    at(scale_x, s, 3)
-                at(widen, s + 2, k, nc.scalar.copy)
-            for k in range(3):
-                at(turn_x, s + 1, k)
+            at(moment, s - LAG - 2, 1)
+            if s > 1:
+                turn_x(s, 2)
+            scale_x(s, 1)
+            turn_x(s, 3)
+            scale_x(s, 2)
+            scale_x(s, 3)
+            if s != 1:
+                widen(s + 1, 0)
+            if s > 0:
+                group_tz(s, scalar_interleave, E + POOL_Z, E + Q)
+            for t in range(PACK):
+                at(residual, s - 1, t)
+                if t == WB and s != 1:
+                    widen(s + 1, 1)
+                if t >= 2:
+                    turn_x(s + 1, t - 2)
+            if s == 0:
+                widen(2, 0)
+                widen(2, 1)
+                prepare_small()
+            quant_x(s, 0)
+            quant_x(s, 1)
             if s == 0:
                 quant_m()
-                prepare_small()
-            at(quant_x, s, 0)
-            at(quant_x, s, 1)
             at(quant_t, s - LAG)
-            at(quant_z, s)
+            if s == 1:
+                quant_z(0, s, 0)
+                quant_z(1, s, Q)
+            if s > 0:
+                quant_z(s + 1, s, E)
+            at(moment, s - LAG - 1, 0)
 
-        last = GROUPS - 1
+        half = PASS // 2
         load_y(last)
-        load_z(GROUPS + 1)
+        load_z(GROUPS)
         for t in range(PACK):
             clip(last - 2, t)
-        residual(last - 1, 0)
-        residual(last - 1, 1)
-        group_tz(GROUPS, vector_interleave, 0, E)
+        group_tz(last, pool_interleave, 0, E)
+        scale_x(last, 0)
         for k in range(CHUNKS):
-            predict(last, k, k == 2)
-        moment(last - 3)
-        quant_t(last - 2)
-        residual(last - 1, 2)
-        residual(last - 1, 3)
+            predict(last - 1, k)
+        turn_x(last, 2)
+        scale_x(last, 1)
+        turn_x(last, 3)
+        scale_x(last, 2)
+        quant_x(last, 0, 0, half)
+        quant_x(last, 1, 0, half)
+        scale_x(last, 3)
+        for t in range(PACK):
+            residual(last - 1, t)
+        quant_x(last, 0, half, PASS)
+        quant_x(last, 1, half, PASS)
+        predict_half(last, 0, 0, False)
+        predict_half(last, 0, 1, False)
         for t in range(PACK):
             clip(last - 1, t)
-        load_z(GROUPS + 2)
-        moment(last - 2)
+        predict_half(last, 1, 0, True)
+        predict_half(last, 1, 1, False)
+        load_z(GROUPS + 1)
         residual(last, 0)
-        group_tz(GROUPS + 1, vector_interleave, 0, E)
         residual(last, 1)
+        group_tz(GROUPS, vector_interleave, 0, E)
+        moment(last - 4, 1)
+        residual(last, 2)
+        quant_t(last - 2)
         clip(last, 0)
         quant_t(last - 1)
-        residual(last, 2)
         clip(last, 1)
-        residual(last, 3, True)
-        moment(last - 1)
+        residual(last, 3)
         clip(last, 2)
         clip(last, 3)
-        group_tz(GROUPS + 2, vector_interleave, 0, TAIL_V)
-        group_tz(GROUPS + 2, scalar_interleave, TAIL_V, E)
+        for j in range(last - 3, last):
+            moment(j, 0)
+            moment(j, 1)
+        group_tz(GROUPS + 1, vector_interleave, 0, TAIL_V)
+        group_tz(GROUPS + 1, scalar_interleave, TAIL_V, E)
         quant_t(last)
-        moment(last)
+        moment(last, 0)
+        moment(last, 1)
 
         result = keep.tile([P, Q // P, E], F32)
         inv = 1.0 / math.sqrt(B)

@@ -25,7 +25,7 @@ CHUNKS = E // P
 RING = 3
 TAIL_V = 336
 LAG = 2
-POOL_Z = 224
+POOL_Z = 240
 WB = 2
 
 
@@ -60,7 +60,10 @@ def tile_iv4rechubermomentmatrix_t_kernel(tc, x_bytes, x_scale, m, b, y, c, z, o
 
         def load_x(j):
             xb[j] = work.tile([P, PACK * D], U8, name="x_fp8_bytes", bufs=3)
-            nc.sync.dma_start(out=xb[j][:], in_=x_rows[j])
+            pieces = 2 if j == 0 else 1
+            width = PACK * D // pieces
+            for i in range(pieces):
+                nc.sync.dma_start(out=xb[j][:, width * i : width * (i + 1)], in_=x_rows[j][:, width * i : width * (i + 1)])
 
         def load_y(j):
             yt[j] = work.tile([P, PACK, E], BF16, name="y_tile", bufs=3)
@@ -109,28 +112,33 @@ def tile_iv4rechubermomentmatrix_t_kernel(tc, x_bytes, x_scale, m, b, y, c, z, o
             nc.scalar.activation(out=lo_c[:], in_=hi_c[:], func=ACT.Copy, scale=-1.0)
 
         def widen(j, h):
-            xw[j, h] = work.tile([P, 2 * D], BF16, name="x_wide", bufs=6)
+            wide = work.tile([P, 2 * D], BF16, name="x_wide", bufs=6)
             codes = xb[j][:, 2 * D * h : 2 * D * (h + 1)].bitcast(FP8)
             nc.scalar.copy(
-                out=xw[j, h][:].rearrange("p (u w e) -> p u w e", u=2, e=2),
+                out=wide[:].rearrange("p (u w e) -> p u w e", u=2, e=2),
                 in_=codes.rearrange("p (w u e) -> p u w e", u=2, e=2),
             )
+            xw[j, h] = wide[:].bitcast(F32).rearrange("p (u r g w) -> p u r g w", u=2, r=2, g=XPASSES)
 
-        def widen_on_vector(j, h):
-            xw[j, h] = work.tile([P, 2 * D], BF16, name="x_wide", bufs=6)
-            codes = xb[j][:, 2 * D * h : 2 * D * (h + 1)].bitcast(FP8)
-            nc.vector.tensor_copy(
-                out=xw[j, h][:].rearrange("p (u w e) -> p w u e", u=2, e=2),
-                in_=codes.rearrange("p (w u e) -> p w u e", u=2, e=2),
+        def widen_first(h):
+            wide = work.tile([P, 2 * D], BF16, name="x_wide", bufs=6)
+            codes = xb[0][:, 2 * D * h : 2 * D * (h + 1)].bitcast(FP8)
+            nc.scalar.copy(
+                out=wide[:, :D].rearrange("p (u w e) -> p u w e", u=2, e=2),
+                in_=codes[:, :D].rearrange("p (w u e) -> p u w e", u=2, e=2),
             )
+            nc.vector.tensor_copy(
+                out=wide[:, D:].rearrange("p (u w e) -> p w u e", u=2, e=2),
+                in_=codes[:, D:].rearrange("p (w u e) -> p w u e", u=2, e=2),
+            )
+            xw[0, h] = wide[:].bitcast(F32).rearrange("p (r u g w) -> p u r g w", u=2, r=2, g=XPASSES)
 
         def turn_x(j, k):
             h, g = divmod(k, 2)
             xt[j, k] = xring.tile([P, 2, 2, P], F32, name="x_bank")
-            words = xw[j, h][:].bitcast(F32).rearrange("p (u r g w) -> p u r g w", u=2, r=2, g=XPASSES)
             for u in range(2):
                 for r in range(2):
-                    nc.tensor.transpose(xt[j, k][:, u, r, :], words[:, u, r, g, :], ident_f32[:])
+                    nc.tensor.transpose(xt[j, k][:, u, r, :], xw[j, h][:, u, r, g, :], ident_f32[:])
 
         def scale_x(j, k):
             h, g = divmod(k, 2)
@@ -244,8 +252,8 @@ def tile_iv4rechubermomentmatrix_t_kernel(tc, x_bytes, x_scale, m, b, y, c, z, o
             if 0 <= j < GROUPS:
                 fn(j, *rest)
 
-        widen(0, 0)
-        widen_on_vector(0, 1)
+        widen_first(0)
+        widen_first(1)
         turn_x(0, 0)
         turn_x(0, 1)
         scalar_interleave(m_grouped[0][:], m_raw[0][:])
@@ -328,7 +336,6 @@ def tile_iv4rechubermomentmatrix_t_kernel(tc, x_bytes, x_scale, m, b, y, c, z, o
         residual(last, 0)
         residual(last, 1)
         group_tz(GROUPS, vector_interleave, 0, E)
-        moment(last - 4, 1)
         residual(last, 2)
         quant_t(last - 2)
         clip(last, 0)
@@ -337,6 +344,7 @@ def tile_iv4rechubermomentmatrix_t_kernel(tc, x_bytes, x_scale, m, b, y, c, z, o
         residual(last, 3)
         clip(last, 2)
         clip(last, 3)
+        moment(last - 4, 1)
         for j in range(last - 3, last):
             moment(j, 0)
             moment(j, 1)
@@ -350,5 +358,5 @@ def tile_iv4rechubermomentmatrix_t_kernel(tc, x_bytes, x_scale, m, b, y, c, z, o
         inv = 1.0 / math.sqrt(B)
         nc.scalar.activation(out=result[:, 0, :], in_=moments[0][:], func=ACT.Copy, scale=inv)
         nc.vector.tensor_scalar(out=result[:, 1, :], in0=moments[1][:], scalar1=inv, scalar2=None, op0=ALU.mult)
-        for h in range(Q // P):
-            nc.sync.dma_start(out=out[P * h : P * (h + 1), :], in_=result[:, h, :])
+        nc.scalar.dma_start(out=out[:P, :], in_=result[:, 0, :])
+        nc.sync.dma_start(out=out[P:, :], in_=result[:, 1, :])

import math
from contextlib import ExitStack

import concourse.mybir as mybir
from concourse.masks import make_identity

B, D, E, Q = 8192, 1024, 512, 256
FLOPS = 2 * B * D * E + 2 * B * Q * E

F32 = mybir.dt.float32
BF16 = mybir.dt.bfloat16
U32 = mybir.dt.uint32
U8 = mybir.dt.uint8
FP8 = mybir.dt.float8_e4m3fn
FP8X4 = mybir.dt.float8_e4m3fn_x4
ACT = mybir.ActivationFunctionType
ALU = mybir.AluOpType

P = 128
PACK = 4
PASS = P * PACK
GROUPS = B // PASS
XPASSES = D // PASS
CHUNKS = E // P
RING = 3
TAIL_V = 336
LAG = 2
POOL_Z = 240
WB = 2


def interleave(copy, dst, src):
    copy(
        out=dst.rearrange("p (c i t) -> p c t i", i=4, t=PACK),
        in_=src.rearrange("p t (c i) -> p c t i", i=4),
    )


def tile_iv4rechubermomentmatrix_t_kernel(tc, x_bytes, x_scale, m, b, y, c, z, out):
    nc = tc.nc
    x_rows = x_bytes.rearrange("(j p t) k -> j p (t k)", p=P, t=PACK)
    y_rows = y.rearrange("(j p t) e -> j p t e", p=P, t=PACK)
    z_rows = z.rearrange("(j p t) q -> j p t q", p=P, t=PACK)
    m_rows = m.rearrange("(g p t) e -> g p t e", p=P, t=PACK)

    with ExitStack() as ctx:
        keep = ctx.enter_context(tc.tile_pool(name="keep", bufs=1))
        work = ctx.enter_context(tc.tile_pool(name="work", bufs=2))
        ring = ctx.enter_context(tc.psum_pool(name="ring", bufs=RING))
        xring = ctx.enter_context(tc.psum_pool(name="xring", bufs=6 - RING))
        sums = ctx.enter_context(tc.psum_pool(name="sums", bufs=1))
        ctx.enter_context(tc.manual_schedule())

        ident_f32 = keep.tile([P, P], F32)
        ident_bf16 = keep.tile([P, P], BF16)
        make_identity(nc, ident_f32[:])
        make_identity(nc, ident_bf16[:])

        xb, xw, xg, xq, xs, yt, zt, zg, zq, zs, wt, tv, tc_, tg, tq, ts, xt = ({} for n in range(17))

        def load_x(j):
            xb[j] = work.tile([P, PACK * D], U8, name="x_fp8_bytes", bufs=3)
            pieces = 2 if j == 0 else 1
            width = PACK * D // pieces
            for i in range(pieces):
                nc.sync.dma_start(out=xb[j][:, width * i : width * (i + 1)], in_=x_rows[j][:, width * i : width * (i + 1)])

        def load_y(j):
            yt[j] = work.tile([P, PACK, E], BF16, name="y_tile", bufs=3)
            nc.sync.dma_start(out=yt[j][:], in_=y_rows[j])

        def load_z(s):
            tc_[s] = work.tile([P, PACK, E + Q], BF16, name="tz_planes", bufs=3)
            if s == 1:
                for j in range(2):
                    nc.sync.dma_start(out=tc_[s][:, :, Q * j : Q * (j + 1)], in_=z_rows[j])
            if s + 1 < GROUPS:
                nc.sync.dma_start(out=tc_[s][:, :, E:], in_=z_rows[s + 1])

        scale_cols = keep.tile([P, XPASSES, PACK], F32)
        load_x(0)
        nc.sync.dma_start(out=scale_cols[:], in_=x_scale.rearrange("o (g p t) -> p (o g) t", p=P, t=PACK))
        m_raw = [keep.tile([P, PACK, E], BF16, name="m_raw%d" % g) for g in range(XPASSES)]
        for g in range(XPASSES):
            nc.sync.dma_start(out=m_raw[g][:], in_=m_rows[g])
        load_x(1)
        b_raw = keep.tile([P, CHUNKS, 2], BF16)
        nc.sync.dma_start(out=b_raw[:, :, 0:1], in_=b.rearrange("(j p o) -> p j o", p=P, o=1), allow_slow_non_contiguous=True)
        load_x(2)
        load_z(1)
        c_raw = keep.tile([P, GROUPS, PACK], BF16)
        nc.sync.dma_start(out=c_raw[:], in_=c.rearrange("(j p t) -> p j t", p=P, t=PACK))

        m_codes = keep.tile([P, XPASSES, E], U32, align_bytes=64)
        m_scales = keep.tile([P, XPASSES, E], U8, align_bytes=64)
        m_grouped = [work.tile([P, PACK * E], BF16, name="tz_grouped", bufs=2, align_bytes=64) for g in range(XPASSES)]
        neg_b = keep.tile([P, CHUNKS], F32)
        neg_c = keep.tile([P, GROUPS * PACK], F32)
        hi_c = keep.tile([P, GROUPS * PACK], F32)
        lo_c = keep.tile([P, GROUPS * PACK], F32)
        moments = [sums.tile([P, E], F32, name="moment%d" % h) for h in range(Q // P)]

        def quant_m():
            for g in reversed(range(XPASSES)):
                nc.vector.quantize_mx(out=m_codes[:, g, :].bitcast(FP8X4), scales=m_scales[:, g, :], in_=m_grouped[g][:])

        def prepare_small():
            c_flat = c_raw[:].rearrange("p j t -> p (j t)")
            nc.scalar.activation(out=neg_b[:], in_=b_raw[:, :, 0], func=ACT.Copy, scale=-1.0)
            nc.scalar.activation(out=neg_c[:], in_=c_flat, func=ACT.Copy, scale=-1.0)
            nc.scalar.activation(out=hi_c[:], in_=c_flat, func=ACT.Abs)
            nc.scalar.activation(out=lo_c[:], in_=hi_c[:], func=ACT.Copy, scale=-1.0)

        def widen(j, h):
            wide = work.tile([P, 2 * D], BF16, name="x_wide", bufs=6)
            codes = xb[j][:, 2 * D * h : 2 * D * (h + 1)].bitcast(FP8)
            nc.scalar.copy(
                out=wide[:].rearrange("p (u w e) -> p u w e", u=2, e=2),
                in_=codes.rearrange("p (w u e) -> p u w e", u=2, e=2),
            )
            xw[j, h] = wide[:].bitcast(F32).rearrange("p (u r g w) -> p u r g w", u=2, r=2, g=XPASSES)

        def widen_first(h):
            wide = work.tile([P, 2 * D], BF16, name="x_wide", bufs=6)
            codes = xb[0][:, 2 * D * h : 2 * D * (h + 1)].bitcast(FP8)
            nc.scalar.copy(
                out=wide[:, :D].rearrange("p (u w e) -> p u w e", u=2, e=2),
                in_=codes[:, :D].rearrange("p (w u e) -> p u w e", u=2, e=2),
            )
            nc.vector.tensor_copy(
                out=wide[:, D:].rearrange("p (u w e) -> p w u e", u=2, e=2),
                in_=codes[:, D:].rearrange("p (w u e) -> p w u e", u=2, e=2),
            )
            xw[0, h] = wide[:].bitcast(F32).rearrange("p (r u g w) -> p u r g w", u=2, r=2, g=XPASSES)

        def turn_x(j, k):
            h, g = divmod(k, 2)
            xt[j, k] = xring.tile([P, 2, 2, P], F32, name="x_bank")
            for u in range(2):
                for r in range(2):
                    nc.tensor.transpose(xt[j, k][:, u, r, :], xw[j, h][:, u, r, g, :], ident_f32[:])

        def scale_x(j, k):
            h, g = divmod(k, 2)
            if h == 0:
                xg[j, g] = work.tile([P, PACK * PASS], BF16, name="x_grouped", bufs=4, align_bytes=64)
            values = xt[j, k][:].rearrange("p u r n -> p (u r n)").bitcast(BF16)
            nc.vector.tensor_tensor(
                out=xg[j, g][:, 2 * PASS * h : 2 * PASS * (h + 1)].rearrange("p (n u e) -> p n u e", u=2, e=2),
                in0=values.rearrange("p (u n e) -> p n u e", u=2, e=2),
                in1=scale_cols[:, g, :].rearrange("p (u e) -> p u e", u=2).unsqueeze(1).to_broadcast([P, 2 * P, 2, 2]),
                op=ALU.mult,
            )

        def quant_x(j, g, lo=0, hi=PASS):
            if lo == 0:
                xq[j, g] = work.tile([P, PASS], U32, name="x_codes", bufs=4, align_bytes=64)
                xs[j, g] = work.tile([P, PASS], U8, name="x_scales", bufs=4, align_bytes=64)
            nc.vector.quantize_mx(out=xq[j, g][:, lo:hi].bitcast(FP8X4), scales=xs[j, g][:, lo:hi], in_=xg[j, g][:, PACK * lo : PACK * hi])

        def predict_into(bank, j, k, lo, hi):
            cols = slice(P * k, P * (k + 1))
            for g in range(XPASSES):
                nc.tensor.matmul_mx(
                    out=bank, lhsT=m_codes[:, g, cols].bitcast(FP8X4), lhsT_scale=m_scales[:, g, cols],
                    rhs=xq[j, g][:, lo:hi].bitcast(FP8X4), rhs_scale=xs[j, g][:, lo:hi], start=(g == 0), stop=(g == XPASSES - 1),
                )

        def add_bias(bank, j, k, lo, hi, on_vector):
            if lo == 0:
                wt[j, k] = work.tile([P, PASS], F32, name="pred_T", bufs=2 * CHUNKS)
            if on_vector:
                nc.vector.tensor_scalar(out=wt[j, k][:, lo:hi], in0=bank, scalar1=-1.0, scalar2=neg_b[:, k : k + 1], op0=ALU.mult, op1=ALU.add)
            else:
                nc.scalar.activation(out=wt[j, k][:, lo:hi], in_=bank, func=ACT.Identity, scale=-1.0, bias=neg_b[:, k : k + 1])

        def predict(j, k):
            bank = ring.tile([P, PASS], F32, name="bank")
            predict_into(bank[:], j, k, 0, PASS)
            add_bias(bank[:], j, k, 0, PASS, False)

        def predict_half(j, h, pair, on_vector):
            half = PASS // 2
            if h == 0:
                bank = ring.tile([P, 2, half], F32, name="bank")
            else:
                bank = xring.tile([P, 2, half], F32, name="x_bank")
            for i in range(2):
                predict_into(bank[:, i, :], j, 2 * pair + i, half * h, half * (h + 1))
            for i in range(2):
                add_bias(bank[:, i, :], j, 2 * pair + i, half * h, half * (h + 1), on_vector)

        def residual(j, t, on_vector=False):
            bank = ring.tile([P, E], F32, name="bank")
            nc.tensor.matmul(out=bank[:], lhsT=ident_bf16[:], rhs=yt[j][:, t, :], start=True, stop=False)
            for k in range(CHUNKS):
                nc.tensor.matmul(
                    out=bank[:, P * k : P * (k + 1)], lhsT=wt[j, k][:, P * t : P * (t + 1)], rhs=ident_f32[:],
                    is_transpose=True, start=False, stop=(k == CHUNKS - 1),
                )
            if t == 0:
                tv[j] = work.tile([P, PACK, E], BF16, name="t_unclipped", bufs=2)
            col = PACK * j + t
            if on_vector:
                nc.vector.tensor_scalar(out=tv[j][:, t, :], in0=bank[:], scalar1=neg_c[:, col : col + 1], scalar2=None, op0=ALU.mult)
            else:
                nc.scalar.activation(out=tv[j][:, t, :], in_=bank[:], func=ACT.Copy, scale=neg_c[:, col : col + 1])

        def clip(j, t):
            col = PACK * j + t
            nc.vector.tensor_scalar(
                out=tc_[j + LAG][:, t, :E], in0=tv[j][:, t, :], scalar1=lo_c[:, col : col + 1], scalar2=hi_c[:, col : col + 1],
                op0=ALU.max, op1=ALU.min,
            )

        def pool_interleave(dst, src):
            nc.gpsimd.tensor_scalar(
                out=dst.rearrange("p (c t) -> p c t", t=PACK), in0=src.rearrange("p t c -> p c t"),
                scalar1=1.0, scalar2=0.0, op0=ALU.mult, op1=ALU.add,
            )

        def group_tz(j, how, lo, hi):
            if j not in tg:
                tg[j] = work.tile([P, PACK * (E + Q)], BF16, name="tz_grouped", bufs=2, align_bytes=64)
            if lo < hi:
                how(tg[j][:, PACK * lo : PACK * hi], tc_[j][:, :, lo:hi])

        def vector_interleave(dst, src):
            interleave(nc.vector.tensor_copy, dst, src)

        def scalar_interleave(dst, src):
            interleave(nc.scalar.copy, dst, src)

        def quant_t(j):
            tq[j] = work.tile([P, E], U32, name="t_codes", bufs=4, align_bytes=64)
            ts[j] = work.tile([P, E], U8, name="t_scales", bufs=4, align_bytes=64)
            nc.vector.quantize_mx(out=tq[j][:].bitcast(FP8X4), scales=ts[j][:], in_=tg[j + LAG][:, : PACK * E])

        def quant_z(j, s, lo):
            zq[j] = work.tile([P, Q], U32, name="z_codes", bufs=7, align_bytes=64)
            zs[j] = work.tile([P, Q], U8, name="z_scales", bufs=7, align_bytes=64)
            nc.vector.quantize_mx(out=zq[j][:].bitcast(FP8X4), scales=zs[j][:], in_=tg[s][:, PACK * lo : PACK * (lo + Q)])

        def moment(j, h):
            cols = slice(P * h, P * (h + 1))
            nc.tensor.matmul_mx(
                out=moments[h][:], lhsT=zq[j][:, cols].bitcast(FP8X4), lhsT_scale=zs[j][:, cols],
                rhs=tq[j][:].bitcast(FP8X4), rhs_scale=ts[j][:], start=(j == 0), stop=(j == GROUPS - 1),
            )

        def at(fn, j, *rest):
            if 0 <= j < GROUPS:
                fn(j, *rest)

        widen_first(0)
        widen_first(1)
        turn_x(0, 0)
        turn_x(0, 1)
        scalar_interleave(m_grouped[0][:], m_raw[0][:])
        pool_interleave(m_grouped[1][:], m_raw[1][:])
        last = GROUPS - 1
        for s in range(last):
            load_y(s)
            if s > 0:
                load_z(s + 1)
                at(load_x, s + 2)
            for t in range(PACK):
                at(clip, s - LAG, t)
            if s > 0:
                group_tz(s, pool_interleave, 0, E + POOL_Z)
            scale_x(s, 0)
            if s <= 1:
                turn_x(s, 2)
            for k in range(CHUNKS):
                at(predict, s - 1, k)
            at(moment, s - LAG - 2, 1)
            if s > 1:
                turn_x(s, 2)
            scale_x(s, 1)
            turn_x(s, 3)
            scale_x(s, 2)
            scale_x(s, 3)
            if s != 1:
                widen(s + 1, 0)
            if s > 0:
                group_tz(s, scalar_interleave, E + POOL_Z, E + Q)
            for t in range(PACK):
                at(residual, s - 1, t)
                if t == WB and s != 1:
                    widen(s + 1, 1)
                if t >= 2:
                    turn_x(s + 1, t - 2)
            if s == 0:
                widen(2, 0)
                widen(2, 1)
                prepare_small()
            quant_x(s, 0)
            quant_x(s, 1)
            if s == 0:
                quant_m()
            at(quant_t, s - LAG)
            if s == 1:
                quant_z(0, s, 0)
                quant_z(1, s, Q)
            if s > 0:
                quant_z(s + 1, s, E)
            at(moment, s - LAG - 1, 0)

        half = PASS // 2
        load_y(last)
        load_z(GROUPS)
        for t in range(PACK):
            clip(last - 2, t)
        group_tz(last, pool_interleave, 0, E)
        scale_x(last, 0)
        for k in range(CHUNKS):
            predict(last - 1, k)
        turn_x(last, 2)
        scale_x(last, 1)
        turn_x(last, 3)
        scale_x(last, 2)
        quant_x(last, 0, 0, half)
        quant_x(last, 1, 0, half)
        scale_x(last, 3)
        for t in range(PACK):
            residual(last - 1, t)
        quant_x(last, 0, half, PASS)
        quant_x(last, 1, half, PASS)
        predict_half(last, 0, 0, False)
        predict_half(last, 0, 1, False)
        for t in range(PACK):
            clip(last - 1, t)
        predict_half(last, 1, 0, True)
        predict_half(last, 1, 1, False)
        load_z(GROUPS + 1)
        residual(last, 0)
        residual(last, 1)
        group_tz(GROUPS, vector_interleave, 0, E)
        residual(last, 2)
        quant_t(last - 2)
        clip(last, 0)
        quant_t(last - 1)
        clip(last, 1)
        residual(last, 3)
        clip(last, 2)
        clip(last, 3)
        moment(last - 4, 1)
        for j in range(last - 3, last):
            moment(j, 0)
            moment(j, 1)
        group_tz(GROUPS + 1, vector_interleave, 0, TAIL_V)
        group_tz(GROUPS + 1, scalar_interleave, TAIL_V, E)
        quant_t(last)
        moment(last, 0)
        moment(last, 1)

        result = keep.tile([P, Q // P, E], F32)
        inv = 1.0 / math.sqrt(B)
        nc.scalar.activation(out=result[:, 0, :], in_=moments[0][:], func=ACT.Copy, scale=inv)
        nc.vector.tensor_scalar(out=result[:, 1, :], in0=moments[1][:], scalar1=inv, scalar2=None, op0=ALU.mult)
        nc.scalar.dma_start(out=out[:P, :], in_=result[:, 0, :])
        nc.sync.dma_start(out=out[P:, :], in_=result[:, 1, :])
